import numpy as np
import ml_dtypes


def mxq(x, axis, fmt="e4m3"):
    dtype, down = {"e4m3": (ml_dtypes.float8_e4m3fn, 7), "e5m2": (ml_dtypes.float8_e5m2, 14)}[fmt]
    v = np.moveaxis(np.asarray(x, np.float32).astype(ml_dtypes.bfloat16).astype(np.float64), axis, -1)
    blocks = v.reshape(v.shape[:-1] + (-1, 32))
    amax = np.abs(blocks).max(-1, keepdims=True)
    byte = np.maximum(np.where(amax > 0, np.frexp(amax)[1] - 1 + 127, 0) - down, 1)
    scale = np.exp2(byte - 127.0)
    codes = (blocks / scale).astype(np.float32).astype(dtype).astype(np.float64)
    return np.moveaxis((codes * scale).reshape(v.shape), -1, axis)


WIDE = False


def mx_kscale(k):
    if not WIDE:
        return np.ones(k)
    levels = np.array([10, -10, 5, -5, 0])
    if k % 512:
        return np.exp2(np.random.permutation(np.resize(levels, k // 32))).repeat(32)
    a = np.empty((k // 512, 16))
    for p in range(k // 512):
        a[p, :8] = np.random.permutation(np.resize(levels, 8))
        for g in range(8):
            far = levels[np.abs(levels - a[p, g]) >= 10]
            a[p, g + 8] = far[np.random.randint(len(far))]
    return np.exp2(a.ravel()).repeat(32)


def f64(x):
    return np.asarray(x).astype(np.float64)


def striped(idx):
    return np.tile(idx.reshape(-1, 16).T, (8, 1)).astype(np.uint16)


def unstriped(offs):
    return offs[:16].T.reshape(-1).astype(np.int64)


E2M1 = np.array([0.0, 0.5, 1.0, 1.5, 2.0, 3.0, 4.0, 6.0, -0.0, -0.5, -1.0, -1.5, -2.0, -3.0, -4.0, -6.0])


def pack_weight(w, fmt):
    k, n = w.shape
    w = f64(np.asarray(w, np.float32).astype(ml_dtypes.bfloat16)).reshape(k // 32, 32, n)
    amax = np.abs(w).max(1)
    if fmt == "e4m3":
        byte = np.frexp(amax)[1] - 1 + 127 - 7
    else:
        mant, ex = np.frexp(amax / 6.0)
        byte = np.where(mant > 0.5, ex, ex - 1) + 127
    byte = np.clip(np.where(amax > 0, byte, 1), 1, 254)
    scaled = (w * np.exp2(127.0 - byte)[:, None, :]).reshape(k, n).astype(np.float32)
    by_word = np.ascontiguousarray(scaled.reshape(k // 512, 128, 4, n).transpose(0, 1, 3, 2))
    if fmt == "e4m3":
        words = by_word.astype(ml_dtypes.float8_e4m3fn).view(np.uint8)
    else:
        c = by_word.astype(ml_dtypes.float4_e2m1fn).view(np.uint8) & 0xF
        words = (c[..., 0::2] | (c[..., 1::2] << 4)).reshape(k // 512, 128, 2 * n)
    return np.ascontiguousarray(words), np.ascontiguousarray(byte.astype(np.uint8).reshape(k // 512, 16, n))


def unpack_weight(words, scales, fmt):
    g, _, n = scales.shape
    words = np.ascontiguousarray(words).reshape(g, 128, n, -1)
    if fmt == "e4m3":
        vals = words.view(ml_dtypes.float8_e4m3fn).astype(np.float64)
    else:
        nib = np.empty((g, 128, n, 4), np.uint8)
        nib[..., 0::2] = words & 0xF
        nib[..., 1::2] = words >> 4
        vals = E2M1[nib]
    vals = vals * np.repeat(np.exp2(scales.astype(np.float64) - 127.0), 8, axis=1)[..., None]
    return vals.transpose(0, 1, 3, 2).reshape(g * 512, n)


def gelu(v):
    return 0.5 * v * (1.0 + np.tanh(np.sqrt(2.0 / np.pi) * (v + 0.044715 * v**3)))


def striped8(idx):
    return np.concatenate([v.reshape(-1, 16).T for v in idx]).astype(np.uint16)


def unstriped8(offs):
    return np.stack([offs[16 * g:16 * g + 16].T.reshape(-1) for g in range(8)]).astype(np.int64)


def heads(h, wgt, idx8):
    r = np.arange(h.shape[0])
    return wgt[r // 4 % 128] * h[r[:, None], idx8[r % 512 // 64]]


K, H, N, T, S, P = 512, 1024, 384, 4096, 2048, 1024

def setup_inputs():
    n = np.random.standard_normal
    s = mx_kscale(K)[:, None]
    u = mx_kscale(H)[:, None]
    tab_words, tab_scales = pack_weight(n((K, T)) * s, "e4m3")
    w4_words, w4_scales = pack_weight(n((K, H)) / np.sqrt(K) / s, "e2m1")
    return {
        "tab_words": tab_words, "tab_scales": tab_scales,
        "offs": striped(np.random.permutation(T)[:S]),
        "offs2": striped8(np.stack([np.random.permutation(S)[:P] for _ in range(8)])),
        "offs3": striped8(np.stack([np.random.permutation(S)[:P] for _ in range(8)])),
        "w1": (n((K, H)) / np.sqrt(K) / s).astype(np.float32),
        "w4_words": w4_words, "w4_scales": w4_scales,
        "gain": (np.exp(0.3 * n(H)) * np.sqrt(u[:, 0])).astype(np.float32),
        "wga": np.repeat(np.random.uniform(0.5, 2.0, (8, P)), 16, axis=0).astype(np.float32),
        "wgb": np.repeat(np.random.uniform(0.5, 2.0, (8, P)), 16, axis=0).astype(np.float32),
        "w2": (0.5 * n((H, N)) / np.sqrt(H) / u).astype(np.float32),
        "tester": n(N).astype(np.float32),
    }

def reference(tab_words, tab_scales, offs, offs2, offs3, w1, w4_words, w4_scales, gain, wga, wgb, w2, tester):
    v = unpack_weight(tab_words, tab_scales, "e4m3")[:, unstriped(offs)]
    w4 = unpack_weight(w4_words, w4_scales, "e2m1")
    ha = mxq(f64(w1), 0, "e4m3").T @ v
    hb = w4.T @ v
    h = np.maximum(ha, hb) * f64(gain)[:, None]
    xa = heads(h, f64(wga), unstriped8(offs2))
    xb = heads(h, f64(wgb), unstriped8(offs3))
    x = xa * xb
    y = mxq(f64(w2), 0, "e4m3").T @ mxq(x, 0, "e4m3")
    return y + f64(tester)[:, None]

@@ -1,0 +1,297 @@
+from contextlib import ExitStack
+
+import concourse.mybir as mybir
+
+K, H, N, T, S, M = 512, 1024, 384, 4096, 2048, 1024
+FLOPS = 2 * (2 * K * H * S + H * N * M)
+
+F32 = mybir.dt.float32
+BF16 = mybir.dt.bfloat16
+I32 = mybir.dt.int32
+U32 = mybir.dt.uint32
+U16 = mybir.dt.uint16
+U8 = mybir.dt.uint8
+FP8X4 = mybir.dt.float8_e4m3fn_x4
+FP4X4 = mybir.dt.float4_e2m1fn_x4
+ALU = mybir.AluOpType
+ACT = mybir.ActivationFunctionType
+
+P = 128
+PACK = 4
+BANK = 512
+PASSES = H // (P * PACK)
+SLICES = H // P
+PER_COL = 16
+N_TILES = N // P
+LAST_PASS_CHUNKS = (512, 256, 128, 128)
+
+
+def tile_list_testcross_heterosis_scores_kernel(
+    tc, tab_words, tab_scales, offs, offs2, offs3, w1, w4_words, w4_scales, gain, wga, wgb, w2, tester, out
+):
+    nc = tc.nc
+    with ExitStack() as ctx:
+        keep = ctx.enter_context(tc.tile_pool(name="keep", bufs=1))
+        ring = ctx.enter_context(tc.tile_pool(name="ring", bufs=1))
+        psum = ctx.enter_context(tc.psum_pool(name="psum", bufs=1))
+
+        def held(name, shape, dtype):
+            return keep.tile(shape, dtype, name=name, align_bytes=64)
+
+        def load_scale_rows(tile, rows):
+            for q in range(4):
+                nc.sync.dma_start(
+                    out=tile[32 * q : 32 * q + 4, :].bitcast(I32), in_=rows[4 * q : 4 * q + 4, :].bitcast(I32)
+                )
+
+        lines = held("lines", [P, S // PER_COL], U16)
+        seeds = held("seeds", [P, M // PER_COL], U16)
+        pollen = held("pollen", [P, M // PER_COL], U16)
+        tab_w = held("tab_w", [P, T], U32)
+        tab_s = held("tab_s", [P, T], U8)
+        w4_w_raw = held("w4_w_raw", [P, 2 * H], U8)
+        w4_s_raw = held("w4_s_raw", [P, H], U8)
+        nc.vector.memset(tab_s[:].bitcast(I32), 0)
+        nc.gpsimd.memset(w4_s_raw[:].bitcast(I32), 0)
+
+        nc.sync.dma_start(out=lines[:], in_=offs)
+        nc.sync.dma_start(out=w4_w_raw[:].bitcast(I32), in_=w4_words[0].bitcast(I32))
+        load_scale_rows(tab_s, tab_scales[0])
+        nc.sync.dma_start(out=tab_w[:].bitcast(I32), in_=tab_words[0].rearrange("p t i -> p (t i)").bitcast(I32))
+        load_scale_rows(w4_s_raw, w4_scales[0])
+
+        w1_rows = w1.rearrange("(p j) r -> p j r", j=PACK)
+        w1_raw = []
+        for piece in range(4):
+            raw = held(f"w1_raw{piece}", [P, PACK, 256], F32)
+            w1_raw.append(raw)
+
+        def load_w1(piece):
+            nc.sync.dma_start(out=w1_raw[piece][:], in_=w1_rows[:, :, 256 * piece : 256 * (piece + 1)])
+
+        load_w1(0)
+        load_w1(1)
+        gain_raw = held("gain_raw", [P, PASSES, PACK], F32)
+        nc.sync.dma_start(out=gain_raw[:], in_=gain.rearrange("(b p t) -> p b t", b=PASSES, t=PACK))
+        weight = held("weight", [P, M], F32)
+        weight_b = held("weight_b", [P, M], F32)
+        nc.sync.dma_start(out=weight[:], in_=wga)
+        nc.sync.dma_start(out=weight_b[:], in_=wgb)
+        nc.sync.dma_start(out=seeds[:], in_=offs2)
+        nc.sync.dma_start(out=pollen[:], in_=offs3)
+        load_w1(2)
+        load_w1(3)
+        w2_raw = []
+        for b in range(PASSES):
+            raw = held(f"w2_raw{b}", [P, PACK, N], F32)
+            nc.sync.dma_start(out=raw[:], in_=w2[BANK * b : BANK * (b + 1), :].rearrange("(p j) n -> p j n", j=PACK))
+            w2_raw.append(raw)
+        tester_col = held("tester_col", [P, N_TILES], F32)
+        with nc.allow_non_contiguous_dma(reason="one value of tester for each partition"):
+            nc.sync.dma_start(out=tester_col[:], in_=tester.rearrange("(c p) -> p c", p=P))
+
+        w4_w = held("w4_w", [P, 2 * H], U8)
+        w4_s = held("w4_s", [P, H], U8)
+        nc.vector.tensor_copy(
+            out=w4_w[:].bitcast(U16).rearrange("p (b t m) -> p b t m", b=PASSES, t=PACK),
+            in_=w4_w_raw[:].bitcast(U16).rearrange("p (b m t) -> p b t m", b=PASSES, t=PACK),
+        )
+
+        v_s = held("v_s", [P, S], U8)
+        nc.vector.tensor_copy(out=v_s[:], in_=tab_s[:].indirect(lines[:]))
+        nc.vector.tensor_copy(
+            out=w4_s[:].rearrange("p (b t m) -> p b t m", b=PASSES, t=PACK),
+            in_=w4_s_raw[:].rearrange("p (b m t) -> p b t m", b=PASSES, t=PACK),
+        )
+        v_w = []
+        for c in range(S // BANK):
+            picked = held(f"v_w{c}", [P, BANK], U32)
+            cols = slice(c * BANK // PER_COL, (c + 1) * BANK // PER_COL)
+            nc.vector.tensor_copy(out=picked[:], in_=tab_w[:].indirect(lines[:, cols]))
+            v_w.append(picked)
+
+        gain_abs = held("gain_abs", [P, SLICES], F32)
+        nc.scalar.activation(out=gain_abs[:], in_=gain_raw[:].rearrange("p b t -> p (b t)"), func=ACT.Abs)
+
+        w1_w, w1_s, w1_bf = [], [], []
+        for b in range(PASSES):
+            w1_w.append(held(f"w1_w{b}", [P, BANK], U32))
+            w1_s.append(held(f"w1_s{b}", [P, BANK], U8))
+            w1_bf.append(held(f"w1_bf{b}", [P, PACK, P, PACK], BF16))
+
+        def round_w1(b):
+            for half in range(2):
+                ms = slice(64 * half, 64 * (half + 1))
+                nc.scalar.copy(
+                    out=w1_bf[b][:, :, ms, :].rearrange("p t m j -> p m j t"),
+                    in_=w1_raw[2 * b + half][:].rearrange("p j (m t) -> p m j t", t=PACK),
+                )
+
+        def quantise_w1(b):
+            nc.vector.quantize_mx(
+                out=w1_w[b][:].bitcast(FP8X4), scales=w1_s[b][:], in_=w1_bf[b][:].rearrange("p t m j -> p (t m j)")
+            )
+
+        def interleave(dst, src, engine_copy):
+            engine_copy(
+                out=dst.rearrange("p (c i t) -> p c t i", i=4, t=PACK),
+                in_=src.rearrange("p t (c i) -> p c t i", i=4),
+            )
+
+        w2_w, w2_s, w2_bf = [], [], []
+        for b in range(PASSES):
+            w2_w.append(held(f"w2_w{b}", [P, N], U32))
+            w2_s.append(held(f"w2_s{b}", [P, N], U8))
+            w2_bf.append(held(f"w2_bf{b}", [P, N * PACK], BF16))
+
+        def quantise_w2(b):
+            nc.vector.quantize_mx(out=w2_w[b][:].bitcast(FP8X4), scales=w2_s[b][:], in_=w2_bf[b][:])
+
+        h = {}
+        readings = {}
+
+        def products(s):
+            b, t = divmod(s, PACK)
+            rows = slice(P * t, P * (t + 1))
+            h[s] = ring.tile([P, S], F32, name="h", tag="h", bufs=6, align_bytes=64)
+            for c in range(S // BANK):
+                cols = slice(BANK * c, BANK * (c + 1))
+                second = psum.tile([P, BANK], F32, name="second", tag="second", bufs=3)
+                nc.tensor.matmul_mx(
+                    out=second[:],
+                    lhsT=w4_w[:, 2 * P * s : 2 * P * (s + 1)].bitcast(FP4X4),
+                    lhsT_scale=w4_s[:, P * s : P * (s + 1)],
+                    rhs=v_w[c][:].bitcast(FP8X4),
+                    rhs_scale=v_s[:, cols],
+                    start=True,
+                    stop=True,
+                )
+                scaled = ring.tile([P, BANK], F32, name="scaled", tag="scaled", bufs=6, align_bytes=64)
+                nc.scalar.activation(out=scaled[:], in_=second[:], func=ACT.Copy, scale=gain_abs[:, s : s + 1])
+                first = psum.tile([P, BANK], F32, name="first", tag="first", bufs=5)
+                nc.tensor.matmul_mx(
+                    out=first[:],
+                    lhsT=w1_w[b][:, rows].bitcast(FP8X4),
+                    lhsT_scale=w1_s[b][:, rows],
+                    rhs=v_w[c][:].bitcast(FP8X4),
+                    rhs_scale=v_s[:, cols],
+                    start=True,
+                    stop=True,
+                )
+                readings[s, c] = (first, scaled)
+
+        def larger(s, cs):
+            for c in cs:
+                first, scaled = readings[s, c]
+                nc.vector.scalar_tensor_tensor(
+                    out=h[s][:, BANK * c : BANK * (c + 1)],
+                    in0=first[:],
+                    scalar=gain_abs[:, s : s + 1],
+                    in1=scaled[:],
+                    op0=ALU.mult,
+                    op1=ALU.max,
+                )
+
+        def seed_side(s, m0, width):
+            xa = ring.tile([P, width], F32, name="xa", tag="xa", bufs=4, align_bytes=64)
+            cols = slice(m0 // PER_COL, (m0 + width) // PER_COL)
+            nc.vector.tensor_tensor(
+                out=xa[:], in0=h[s][:].indirect(seeds[:, cols]), in1=weight[:, m0 : m0 + width], op=ALU.mult
+            )
+            return xa
+
+        def pollen_side(s, m0, width, xa, dst):
+            cols = slice(m0 // PER_COL, (m0 + width) // PER_COL)
+            nc.vector.tensor_tensor(out=dst, in0=h[s][:].indirect(pollen[:, cols]), in1=xa[:], op=ALU.mult)
+
+        x_w = [held(f"x_w{b}", [P, M], U32) for b in range(PASSES)]
+        x_s = [held(f"x_s{b}", [P, M], U8) for b in range(PASSES)]
+
+        def round_x(src, width, engine_copy):
+            x_bf = ring.tile([P, PACK * width], BF16, name="x_bf", tag="x_bf", bufs=2, align_bytes=64)
+            interleave(x_bf[:], src, engine_copy)
+            return x_bf
+
+        def quantise_x(b, m0, width, x_bf):
+            cols = slice(m0, m0 + width)
+            nc.vector.quantize_mx(out=x_w[b][:, cols].bitcast(FP8X4), scales=x_s[b][:, cols], in_=x_bf[:])
+
+        out_rows = out.rearrange("(c p) m -> p c m", p=P)
+
+        def scores(m0, width):
+            cols = slice(m0, m0 + width)
+            accs = [psum.tile([P, width], F32, name="acc", tag="first", bufs=5) for c in range(N_TILES)]
+            for b in range(PASSES):
+                for c in range(N_TILES):
+                    ns = slice(P * c, P * (c + 1))
+                    nc.tensor.matmul_mx(
+                        out=accs[c][:],
+                        lhsT=w2_w[b][:, ns].bitcast(FP8X4),
+                        lhsT_scale=w2_s[b][:, ns],
+                        rhs=x_w[b][:, cols].bitcast(FP8X4),
+                        rhs_scale=x_s[b][:, cols],
+                        start=(b == 0),
+                        stop=(b == PASSES - 1),
+                    )
+            res = held(f"res{m0}", [P, N_TILES, width], F32)
+            for c in range(N_TILES):
+                nc.scalar.activation(
+                    out=res[:, c, :], in_=accs[c][:], func=ACT.Identity, bias=tester_col[:, c : c + 1], scale=1.0
+                )
+            nc.sync.dma_start(out=out_rows[:, :, cols], in_=res[:])
+
+        round_w1(0)
+        quantise_w1(0)
+        nc.vector.tensor_tensor(out=weight[:], in0=weight[:], in1=weight_b[:], op=ALU.mult)
+        products(0)
+        larger(0, range(4))
+        products(1)
+        round_w1(1)
+        larger(1, range(4))
+
+        x0 = held("x0", [P, PACK, M], F32)
+        for s in range(PACK):
+            products(s + 2)
+            if s == 0:
+                quantise_w1(1)
+            if s in (1, 2):
+                interleave(w2_bf[s - 1][:], w2_raw[s - 1][:], nc.scalar.copy)
+            xa = seed_side(s, 0, M)
+            larger(s + 2, (0, 1))
+            pollen_side(s, 0, M, xa, x0[:, s, :])
+            larger(s + 2, (2, 3))
+
+        width = LAST_PASS_CHUNKS[0]
+        x1 = [held(f"x1_{i}", [P, PACK, w], F32) for i, w in enumerate(LAST_PASS_CHUNKS)]
+        products(6)
+        x0_bf = [round_x(x0[:, :, BANK * i : BANK * (i + 1)], BANK, nc.scalar.copy) for i in range(2)]
+        xa4 = seed_side(4, 0, width)
+        xa5 = seed_side(5, 0, width)
+        larger(6, (0, 1))
+        pollen_side(4, 0, width, xa4, x1[0][:, 0, :])
+        larger(6, (2, 3))
+        products(7)
+        pollen_side(5, 0, width, xa5, x1[0][:, 1, :])
+        xa6 = seed_side(6, 0, width)
+        quantise_w2(0)
+        quantise_w2(1)
+        pollen_side(6, 0, width, xa6, x1[0][:, 2, :])
+        larger(7, range(4))
+        quantise_x(0, 0, BANK, x0_bf[0])
+        xa7 = seed_side(7, 0, width)
+        quantise_x(0, BANK, BANK, x0_bf[1])
+        pollen_side(7, 0, width, xa7, x1[0][:, 3, :])
+
+        starts = [sum(LAST_PASS_CHUNKS[:i]) for i in range(len(LAST_PASS_CHUNKS))]
+        pending = (starts[0], width, round_x(x1[0][:], width, nc.scalar.copy))
+        for i in range(1, len(LAST_PASS_CHUNKS)):
+            m0, width = starts[i], LAST_PASS_CHUNKS[i]
+            xas = [seed_side(PACK + t, m0, width) for t in range(PACK)]
+            for t in range(PACK):
+                pollen_side(PACK + t, m0, width, xas[t], x1[i][:, t, :])
+            quantise_x(1, *pending)
+            scores(pending[0], pending[1])
+            last = i == len(LAST_PASS_CHUNKS) - 1
+            pending = (m0, width, round_x(x1[i][:], width, nc.vector.tensor_copy if last else nc.scalar.copy))
+        quantise_x(1, *pending)
+        scores(pending[0], pending[1])

@@ -38,27 +38,29 @@ def tile_list_testcross_heterosis_scores_kernel(
         def held(name, shape, dtype):
             return keep.tile(shape, dtype, name=name, align_bytes=64)
 
-        def load_scale_rows(tile, rows):
+        def reused(name, shape, dtype, buffer):
+            return ring.tile(shape, dtype, name=name, tag=buffer, bufs=1, align_bytes=64)
+
+        def load_scale_rows(queue, tile, rows):
             for q in range(4):
-                nc.sync.dma_start(
-                    out=tile[32 * q : 32 * q + 4, :].bitcast(I32), in_=rows[4 * q : 4 * q + 4, :].bitcast(I32)
+                queue.dma_start(
+                    out=tile[32 * q : 32 * (q + 1), :].bitcast(I32),
+                    in_=rows[4 * q : 4 * q + 4, :].bitcast(I32).partition_broadcast(8),
                 )
 
         lines = held("lines", [P, S // PER_COL], U16)
         seeds = held("seeds", [P, M // PER_COL], U16)
         pollen = held("pollen", [P, M // PER_COL], U16)
-        tab_w = held("tab_w", [P, T], U32)
+        tab_w = reused("tab_w", [P, T], U32, "table")
         tab_s = held("tab_s", [P, T], U8)
-        w4_w_raw = held("w4_w_raw", [P, 2 * H], U8)
-        w4_s_raw = held("w4_s_raw", [P, H], U8)
-        nc.vector.memset(tab_s[:].bitcast(I32), 0)
-        nc.gpsimd.memset(w4_s_raw[:].bitcast(I32), 0)
+        w4_w_raw = reused("w4_w_raw", [P, 2 * H], U8, "picked1")
+        w4_s_raw = reused("w4_s_raw", [P, H], U8, "picked2")
 
         nc.sync.dma_start(out=lines[:], in_=offs)
-        nc.sync.dma_start(out=w4_w_raw[:].bitcast(I32), in_=w4_words[0].bitcast(I32))
-        load_scale_rows(tab_s, tab_scales[0])
+        load_scale_rows(nc.sync, tab_s, tab_scales[0])
         nc.sync.dma_start(out=tab_w[:].bitcast(I32), in_=tab_words[0].rearrange("p t i -> p (t i)").bitcast(I32))
-        load_scale_rows(w4_s_raw, w4_scales[0])
+        nc.sync.dma_start(out=w4_w_raw[:].bitcast(I32), in_=w4_words[0].bitcast(I32))
+        load_scale_rows(nc.sync, w4_s_raw, w4_scales[0])
 
         w1_rows = w1.rearrange("(p j) r -> p j r", j=PACK)
         w1_raw = []
@@ -73,9 +75,9 @@ def tile_list_testcross_heterosis_scores_kernel(
         load_w1(1)
         gain_raw = held("gain_raw", [P, PASSES, PACK], F32)
         nc.sync.dma_start(out=gain_raw[:], in_=gain.rearrange("(b p t) -> p b t", b=PASSES, t=PACK))
-        weight = held("weight", [P, M], F32)
+        weight_a = held("weight_a", [P, M], F32)
         weight_b = held("weight_b", [P, M], F32)
-        nc.sync.dma_start(out=weight[:], in_=wga)
+        nc.sync.dma_start(out=weight_a[:], in_=wga)
         nc.sync.dma_start(out=weight_b[:], in_=wgb)
         nc.sync.dma_start(out=seeds[:], in_=offs2)
         nc.sync.dma_start(out=pollen[:], in_=offs3)
@@ -92,23 +94,27 @@ def tile_list_testcross_heterosis_scores_kernel(
 
         w4_w = held("w4_w", [P, 2 * H], U8)
         w4_s = held("w4_s", [P, H], U8)
+
+        v_s = held("v_s", [P, S], U8)
+        nc.vector.tensor_copy(out=v_s[:], in_=tab_s[:].indirect(lines[:]))
         nc.vector.tensor_copy(
             out=w4_w[:].bitcast(U16).rearrange("p (b t m) -> p b t m", b=PASSES, t=PACK),
             in_=w4_w_raw[:].bitcast(U16).rearrange("p (b m t) -> p b t m", b=PASSES, t=PACK),
         )
-
-        v_s = held("v_s", [P, S], U8)
-        nc.vector.tensor_copy(out=v_s[:], in_=tab_s[:].indirect(lines[:]))
         nc.vector.tensor_copy(
             out=w4_s[:].rearrange("p (b t m) -> p b t m", b=PASSES, t=PACK),
             in_=w4_s_raw[:].rearrange("p (b m t) -> p b t m", b=PASSES, t=PACK),
         )
         v_w = []
-        for c in range(S // BANK):
-            picked = held(f"v_w{c}", [P, BANK], U32)
+
+        def pick_words(c):
+            picked = reused("v_w", [P, BANK], U32, f"picked{c}")
             cols = slice(c * BANK // PER_COL, (c + 1) * BANK // PER_COL)
             nc.vector.tensor_copy(out=picked[:], in_=tab_w[:].indirect(lines[:, cols]))
             v_w.append(picked)
+
+        for c in range(3):
+            pick_words(c)
 
         gain_abs = held("gain_abs", [P, SLICES], F32)
         nc.scalar.activation(out=gain_abs[:], in_=gain_raw[:].rearrange("p b t -> p (b t)"), func=ACT.Abs)
@@ -117,7 +123,7 @@ def tile_list_testcross_heterosis_scores_kernel(
         for b in range(PASSES):
             w1_w.append(held(f"w1_w{b}", [P, BANK], U32))
             w1_s.append(held(f"w1_s{b}", [P, BANK], U8))
-            w1_bf.append(held(f"w1_bf{b}", [P, PACK, P, PACK], BF16))
+            w1_bf.append(reused("w1_bf", [P, PACK, P, PACK], BF16, "picked3" if b == 0 else "w1_bf1"))
 
         def round_w1(b):
             for half in range(2):
@@ -127,9 +133,12 @@ def tile_list_testcross_heterosis_scores_kernel(
                     in_=w1_raw[2 * b + half][:].rearrange("p j (m t) -> p m j t", t=PACK),
                 )
 
-        def quantise_w1(b):
+        def quantise_w1(b, t0, t1):
+            rows = slice(P * t0, P * t1)
             nc.vector.quantize_mx(
-                out=w1_w[b][:].bitcast(FP8X4), scales=w1_s[b][:], in_=w1_bf[b][:].rearrange("p t m j -> p (t m j)")
+                out=w1_w[b][:, rows].bitcast(FP8X4),
+                scales=w1_s[b][:, rows],
+                in_=w1_bf[b][:, t0:t1].rearrange("p t m j -> p (t m j)"),
             )
 
         def interleave(dst, src, engine_copy):
@@ -192,8 +201,8 @@ def tile_list_testcross_heterosis_scores_kernel(
                     op1=ALU.max,
                 )
 
-        def seed_side(s, m0, width):
-            xa = ring.tile([P, width], F32, name="xa", tag="xa", bufs=4, align_bytes=64)
+        def seed_side(s, m0, width, buffer="xa", bufs=4):
+            xa = ring.tile([P, width], F32, name="xa", tag=buffer, bufs=bufs, align_bytes=64)
             cols = slice(m0 // PER_COL, (m0 + width) // PER_COL)
             nc.vector.tensor_tensor(
                 out=xa[:], in0=h[s][:].indirect(seeds[:, cols]), in1=weight[:, m0 : m0 + width], op=ALU.mult
@@ -207,8 +216,8 @@ def tile_list_testcross_heterosis_scores_kernel(
         x_w = [held(f"x_w{b}", [P, M], U32) for b in range(PASSES)]
         x_s = [held(f"x_s{b}", [P, M], U8) for b in range(PASSES)]
 
-        def round_x(src, width, engine_copy):
-            x_bf = ring.tile([P, PACK * width], BF16, name="x_bf", tag="x_bf", bufs=2, align_bytes=64)
+        def round_x(src, width, engine_copy, tag="x_bf", bufs=2):
+            x_bf = ring.tile([P, PACK * width], BF16, name="x_bf", tag=tag, bufs=bufs, align_bytes=64)
             interleave(x_bf[:], src, engine_copy)
             return x_bf
 
@@ -218,31 +227,53 @@ def tile_list_testcross_heterosis_scores_kernel(
 
         out_rows = out.rearrange("(c p) m -> p c m", p=P)
 
-        def scores(m0, width):
+        def score_banks(width, tag, bufs):
+            per_bank = min(N_TILES, BANK // width)
+            accs = []
+            for c0 in range(0, N_TILES, per_bank):
+                count = min(per_bank, N_TILES - c0)
+                bank = psum.tile([P, count, width], F32, name="acc", tag=tag, bufs=bufs)
+                accs.append((bank, c0, count))
+            return accs
+
+        def score_pass(b, m0, width, accs):
             cols = slice(m0, m0 + width)
-            accs = [psum.tile([P, width], F32, name="acc", tag="first", bufs=5) for c in range(N_TILES)]
-            for b in range(PASSES):
-                for c in range(N_TILES):
-                    ns = slice(P * c, P * (c + 1))
+            for bank, c0, count in accs:
+                for i in range(count):
+                    ns = slice(P * (c0 + i), P * (c0 + i + 1))
                     nc.tensor.matmul_mx(
-                        out=accs[c][:],
+                        out=bank[:, i, :],
                         lhsT=w2_w[b][:, ns].bitcast(FP8X4),
                         lhsT_scale=w2_s[b][:, ns],
                         rhs=x_w[b][:, cols].bitcast(FP8X4),
                         rhs_scale=x_s[b][:, cols],
-                        start=(b == 0),
-                        stop=(b == PASSES - 1),
+                        start=(b == 0 and i == 0),
+                        stop=(b == PASSES - 1 and i == count - 1),
                     )
+
+        def store_scores(m0, width, accs, on_vector):
             res = held(f"res{m0}", [P, N_TILES, width], F32)
-            for c in range(N_TILES):
-                nc.scalar.activation(
-                    out=res[:, c, :], in_=accs[c][:], func=ACT.Identity, bias=tester_col[:, c : c + 1], scale=1.0
-                )
-            nc.sync.dma_start(out=out_rows[:, :, cols], in_=res[:])
+            for bank, c0, count in accs:
+                if on_vector:
+                    nc.vector.tensor_tensor(
+                        out=res[:, c0 : c0 + count, :],
+                        in0=bank[:],
+                        in1=tester_col[:, c0 : c0 + count].unsqueeze(2).to_broadcast([P, count, width]),
+                        op=ALU.add,
+                    )
+                else:
+                    for i in range(count):
+                        c = c0 + i
+                        nc.scalar.activation(
+                            out=res[:, c, :], in_=bank[:, i, :], func=ACT.Identity, bias=tester_col[:, c : c + 1], scale=1.0
+                        )
+            nc.sync.dma_start(out=out_rows[:, :, m0 : m0 + width], in_=res[:])
 
         round_w1(0)
-        quantise_w1(0)
-        nc.vector.tensor_tensor(out=weight[:], in0=weight[:], in1=weight_b[:], op=ALU.mult)
+        quantise_w1(0, 0, 4)
+        pick_words(3)
+        weight = reused("weight", [P, M], F32, "table")
+        nc.gpsimd.tensor_tensor(out=weight[:], in0=weight_a[:], in1=weight_b[:], op=ALU.mult)
         products(0)
         larger(0, range(4))
         products(1)
@@ -253,7 +284,7 @@ def tile_list_testcross_heterosis_scores_kernel(
         for s in range(PACK):
             products(s + 2)
             if s == 0:
-                quantise_w1(1)
+                quantise_w1(1, 0, 4)
             if s in (1, 2):
                 interleave(w2_bf[s - 1][:], w2_raw[s - 1][:], nc.scalar.copy)
             xa = seed_side(s, 0, M)
@@ -262,7 +293,7 @@ def tile_list_testcross_heterosis_scores_kernel(
             larger(s + 2, (2, 3))
 
         width = LAST_PASS_CHUNKS[0]
-        x1 = [held(f"x1_{i}", [P, PACK, w], F32) for i, w in enumerate(LAST_PASS_CHUNKS)]
+        x1 = {0: held("x1_0", [P, PACK, width], F32)}
         products(6)
         x0_bf = [round_x(x0[:, :, BANK * i : BANK * (i + 1)], BANK, nc.scalar.copy) for i in range(2)]
         xa4 = seed_side(4, 0, width)
@@ -283,15 +314,50 @@ def tile_list_testcross_heterosis_scores_kernel(
         pollen_side(7, 0, width, xa7, x1[0][:, 3, :])
 
         starts = [sum(LAST_PASS_CHUNKS[:i]) for i in range(len(LAST_PASS_CHUNKS))]
-        pending = (starts[0], width, round_x(x1[0][:], width, nc.scalar.copy))
-        for i in range(1, len(LAST_PASS_CHUNKS)):
-            m0, width = starts[i], LAST_PASS_CHUNKS[i]
-            xas = [seed_side(PACK + t, m0, width) for t in range(PACK)]
-            for t in range(PACK):
-                pollen_side(PACK + t, m0, width, xas[t], x1[i][:, t, :])
-            quantise_x(1, *pending)
-            scores(pending[0], pending[1])
-            last = i == len(LAST_PASS_CHUNKS) - 1
-            pending = (m0, width, round_x(x1[i][:], width, nc.vector.tensor_copy if last else nc.scalar.copy))
-        quantise_x(1, *pending)
-        scores(pending[0], pending[1])
+        banks = []
+        for m0, w in zip(starts, LAST_PASS_CHUNKS):
+            banks.append(score_banks(w, "first", 5) if w > P else score_banks(w, "second", 3))
+            score_pass(0, m0, w, banks[-1])
+
+        def finish(i, x_bf):
+            quantise_x(1, starts[i], LAST_PASS_CHUNKS[i], x_bf)
+            score_pass(1, starts[i], LAST_PASS_CHUNKS[i], banks[i])
+
+        def store(i, on_vector=False):
+            store_scores(starts[i], LAST_PASS_CHUNKS[i], banks[i], on_vector)
+
+        def seeds_of(i, ts, first_buffer=None):
+            xas = {}
+            for t in ts:
+                if first_buffer and t == ts[0]:
+                    xas[t] = seed_side(PACK + t, starts[i], LAST_PASS_CHUNKS[i], first_buffer, 1)
+                else:
+                    xas[t] = seed_side(PACK + t, starts[i], LAST_PASS_CHUNKS[i])
+            return xas
+
+        def pollen_of(i, xas):
+            for t in xas:
+                pollen_side(PACK + t, starts[i], LAST_PASS_CHUNKS[i], xas[t], x1[i][:, t, :])
+
+        bf0 = round_x(x1[0][:], LAST_PASS_CHUNKS[0], nc.scalar.copy, "tail0", 1)
+        x1[1] = held("x1_1", [P, PACK, LAST_PASS_CHUNKS[1]], F32)
+        pollen_of(1, seeds_of(1, (0, 1)))
+        xas = seeds_of(1, (2,))
+        finish(0, bf0)
+        xas[3] = seeds_of(1, (3,), "tail0")[3]
+        pollen_of(1, xas)
+        store(0)
+        bf1 = round_x(x1[1][:], LAST_PASS_CHUNKS[1], nc.scalar.copy, "tail1", 1)
+        x1[2] = held("x1_2", [P, PACK, LAST_PASS_CHUNKS[2]], F32)
+        pollen_of(2, seeds_of(2, (0, 1, 2, 3)))
+        bf2 = round_x(x1[2][:], LAST_PASS_CHUNKS[2], nc.scalar.copy, "tail2", 1)
+        finish(1, bf1)
+        xas = seeds_of(3, (0, 1, 2, 3), "tail1")
+        store(1)
+        finish(2, bf2)
+        x1[3] = reused("x1_3", [P, PACK, LAST_PASS_CHUNKS[3]], F32, "tail2")
+        pollen_of(3, xas)
+        store(2)
+        bf3 = round_x(x1[3][:], LAST_PASS_CHUNKS[3], nc.vector.tensor_copy, "tail3", 1)
+        finish(3, bf3)
+        store(3, True)

@@ -1,6 +1,7 @@
 from contextlib import ExitStack
 
 import concourse.mybir as mybir
+from concourse.masks import make_identity
 
 K, H, N, T, S, M = 512, 1024, 384, 4096, 2048, 1024
 FLOPS = 2 * (2 * K * H * S + H * N * M)
@@ -23,7 +24,10 @@ PASSES = H // (P * PACK)
 SLICES = H // P
 PER_COL = 16
 N_TILES = N // P
-LAST_PASS_CHUNKS = (512, 256, 128, 128)
+W1_PIECE = 256
+CHUNKS = (512, 256, 128, 128)
+TURNED = 7
+TURNED_AT = {0: (0, 1), 1: (2, 3, 4), 2: (5, 6)}
 
 
 def tile_list_testcross_heterosis_scores_kernel(
@@ -41,48 +45,48 @@ def tile_list_testcross_heterosis_scores_kernel(
         def reused(name, shape, dtype, buffer):
             return ring.tile(shape, dtype, name=name, tag=buffer, bufs=1, align_bytes=64)
 
-        def load_scale_rows(queue, tile, rows):
-            for q in range(4):
-                queue.dma_start(
-                    out=tile[32 * q : 32 * (q + 1), :].bitcast(I32),
-                    in_=rows[4 * q : 4 * q + 4, :].bitcast(I32).partition_broadcast(8),
-                )
-
         lines = held("lines", [P, S // PER_COL], U16)
         seeds = held("seeds", [P, M // PER_COL], U16)
         pollen = held("pollen", [P, M // PER_COL], U16)
         tab_w = reused("tab_w", [P, T], U32, "table")
         tab_s = held("tab_s", [P, T], U8)
-        w4_w_raw = reused("w4_w_raw", [P, 2 * H], U8, "picked1")
-        w4_s_raw = reused("w4_s_raw", [P, H], U8, "picked2")
+        w4_w_raw = reused("w4_w_raw", [P, 2 * H], U8, "tail1")
+        w4_s_raw = held("w4_s_raw", [P, H], U8)
+        nc.gpsimd.memset(w4_s_raw[:].bitcast(I32), 0)
+        identity = held("identity", [P, P], F32)
+        make_identity(nc, identity[:])
 
         nc.sync.dma_start(out=lines[:], in_=offs)
-        load_scale_rows(nc.sync, tab_s, tab_scales[0])
+        for q in range(4):
+            nc.sync.dma_start(
+                out=tab_s[32 * q : 32 * (q + 1), :].bitcast(I32),
+                in_=tab_scales[0, 4 * q : 4 * q + 4, :].bitcast(I32).partition_broadcast(8),
+            )
         nc.sync.dma_start(out=tab_w[:].bitcast(I32), in_=tab_words[0].rearrange("p t i -> p (t i)").bitcast(I32))
-        nc.sync.dma_start(out=w4_w_raw[:].bitcast(I32), in_=w4_words[0].bitcast(I32))
-        load_scale_rows(nc.sync, w4_s_raw, w4_scales[0])
 
         w1_rows = w1.rearrange("(p j) r -> p j r", j=PACK)
-        w1_raw = []
-        for piece in range(4):
-            raw = held(f"w1_raw{piece}", [P, PACK, 256], F32)
-            w1_raw.append(raw)
+        w1_raw = [reused("w1_raw", [P, PACK, W1_PIECE], F32, f"w1_raw{piece}") for piece in range(H // W1_PIECE)]
 
-        def load_w1(piece):
-            nc.sync.dma_start(out=w1_raw[piece][:], in_=w1_rows[:, :, 256 * piece : 256 * (piece + 1)])
+        def load_w1(b):
+            for piece in (2 * b, 2 * b + 1):
+                cols = slice(W1_PIECE * piece, W1_PIECE * (piece + 1))
+                nc.sync.dma_start(out=w1_raw[piece][:], in_=w1_rows[:, :, cols])
 
         load_w1(0)
-        load_w1(1)
+        nc.sync.dma_start(out=w4_w_raw[:].bitcast(I32), in_=w4_words[0].bitcast(I32))
+        for q in range(4):
+            nc.sync.dma_start(
+                out=w4_s_raw[32 * q : 32 * q + 4, :].bitcast(I32), in_=w4_scales[0, 4 * q : 4 * q + 4, :].bitcast(I32)
+            )
         gain_raw = held("gain_raw", [P, PASSES, PACK], F32)
         nc.sync.dma_start(out=gain_raw[:], in_=gain.rearrange("(b p t) -> p b t", b=PASSES, t=PACK))
-        weight_a = held("weight_a", [P, M], F32)
-        weight_b = held("weight_b", [P, M], F32)
+        weight_a = reused("weight_a", [P, M], F32, "weight_a")
+        weight_b = reused("weight_b", [P, M], F32, "weight_b")
         nc.sync.dma_start(out=weight_a[:], in_=wga)
         nc.sync.dma_start(out=weight_b[:], in_=wgb)
         nc.sync.dma_start(out=seeds[:], in_=offs2)
         nc.sync.dma_start(out=pollen[:], in_=offs3)
-        load_w1(2)
-        load_w1(3)
+        load_w1(1)
         w2_raw = []
         for b in range(PASSES):
             raw = held(f"w2_raw{b}", [P, PACK, N], F32)
@@ -92,19 +96,8 @@ def tile_list_testcross_heterosis_scores_kernel(
         with nc.allow_non_contiguous_dma(reason="one value of tester for each partition"):
             nc.sync.dma_start(out=tester_col[:], in_=tester.rearrange("(c p) -> p c", p=P))
 
-        w4_w = held("w4_w", [P, 2 * H], U8)
-        w4_s = held("w4_s", [P, H], U8)
-
         v_s = held("v_s", [P, S], U8)
         nc.vector.tensor_copy(out=v_s[:], in_=tab_s[:].indirect(lines[:]))
-        nc.vector.tensor_copy(
-            out=w4_w[:].bitcast(U16).rearrange("p (b t m) -> p b t m", b=PASSES, t=PACK),
-            in_=w4_w_raw[:].bitcast(U16).rearrange("p (b m t) -> p b t m", b=PASSES, t=PACK),
-        )
-        nc.vector.tensor_copy(
-            out=w4_s[:].rearrange("p (b t m) -> p b t m", b=PASSES, t=PACK),
-            in_=w4_s_raw[:].rearrange("p (b m t) -> p b t m", b=PASSES, t=PACK),
-        )
         v_w = []
 
         def pick_words(c):
@@ -113,32 +106,40 @@ def tile_list_testcross_heterosis_scores_kernel(
             nc.vector.tensor_copy(out=picked[:], in_=tab_w[:].indirect(lines[:, cols]))
             v_w.append(picked)
 
-        for c in range(3):
-            pick_words(c)
+        pick_words(0)
+        pick_words(1)
+        pick_words(2)
+        w4_w = held("w4_w", [P, 2 * H], U8)
+        w4_s = held("w4_s", [P, H], U8)
+        nc.vector.tensor_copy(
+            out=w4_w[:].bitcast(U16).rearrange("p (b t m) -> p b t m", b=PASSES, t=PACK),
+            in_=w4_w_raw[:].bitcast(U16).rearrange("p (b m t) -> p b t m", b=PASSES, t=PACK),
+        )
+        nc.vector.tensor_copy(
+            out=w4_s[:].rearrange("p (b t m) -> p b t m", b=PASSES, t=PACK),
+            in_=w4_s_raw[:].rearrange("p (b m t) -> p b t m", b=PASSES, t=PACK),
+        )
 
         gain_abs = held("gain_abs", [P, SLICES], F32)
-        nc.scalar.activation(out=gain_abs[:], in_=gain_raw[:].rearrange("p b t -> p (b t)"), func=ACT.Abs)
+        gain_w1 = held("gain_w1", [P, SLICES], F32)
 
-        w1_w, w1_s, w1_bf = [], [], []
-        for b in range(PASSES):
-            w1_w.append(held(f"w1_w{b}", [P, BANK], U32))
-            w1_s.append(held(f"w1_s{b}", [P, BANK], U8))
-            w1_bf.append(reused("w1_bf", [P, PACK, P, PACK], BF16, "picked3" if b == 0 else "w1_bf1"))
+        w1_w = [held(f"w1_w{b}", [P, BANK], U32) for b in range(PASSES)]
+        w1_s = [held(f"w1_s{b}", [P, BANK], U8) for b in range(PASSES)]
+        w1_bf = [reused("w1_bf", [P, PACK, P, PACK], BF16, buffer) for buffer in ("picked3", "w1_bf")]
 
         def round_w1(b):
             for half in range(2):
-                ms = slice(64 * half, 64 * (half + 1))
-                nc.scalar.copy(
-                    out=w1_bf[b][:, :, ms, :].rearrange("p t m j -> p m j t"),
-                    in_=w1_raw[2 * b + half][:].rearrange("p j (m t) -> p m j t", t=PACK),
+                ms = slice(P // 2 * half, P // 2 * (half + 1))
+                nc.scalar.activation(
+                    out=w1_bf[b][:, :, ms, :].rearrange("p t m j -> p m t j"),
+                    in_=w1_raw[2 * b + half][:].rearrange("p j (m t) -> p m t j", t=PACK),
+                    func=ACT.Copy,
+                    scale=(1.0, -1.0)[b],
                 )
 
-        def quantise_w1(b, t0, t1):
-            rows = slice(P * t0, P * t1)
+        def quantise_w1(b):
             nc.vector.quantize_mx(
-                out=w1_w[b][:, rows].bitcast(FP8X4),
-                scales=w1_s[b][:, rows],
-                in_=w1_bf[b][:, t0:t1].rearrange("p t m j -> p (t m j)"),
+                out=w1_w[b][:].bitcast(FP8X4), scales=w1_s[b][:], in_=w1_bf[b][:].rearrange("p t m j -> p (t m j)")
             )
 
         def interleave(dst, src, engine_copy):
@@ -147,11 +148,9 @@ def tile_list_testcross_heterosis_scores_kernel(
                 in_=src.rearrange("p t (c i) -> p c t i", i=4),
             )
 
-        w2_w, w2_s, w2_bf = [], [], []
-        for b in range(PASSES):
-            w2_w.append(held(f"w2_w{b}", [P, N], U32))
-            w2_s.append(held(f"w2_s{b}", [P, N], U8))
-            w2_bf.append(held(f"w2_bf{b}", [P, N * PACK], BF16))
+        w2_w = [held(f"w2_w{b}", [P, N], U32) for b in range(PASSES)]
+        w2_s = [held(f"w2_s{b}", [P, N], U8) for b in range(PASSES)]
+        w2_bf = [held(f"w2_bf{b}", [P, N * PACK], BF16) for b in range(PASSES)]
 
         def quantise_w2(b):
             nc.vector.quantize_mx(out=w2_w[b][:].bitcast(FP8X4), scales=w2_s[b][:], in_=w2_bf[b][:])
@@ -159,101 +158,155 @@ def tile_list_testcross_heterosis_scores_kernel(
         h = {}
         readings = {}
 
+        def plain_width(s, c):
+            plain = S - (TURNED * P if s >= PACK else 0)
+            return max(0, min(BANK, plain - BANK * c))
+
+        def new_h(s):
+            h[s] = ring.tile([P, S], F32, name="h", tag="h", bufs=6, align_bytes=64)
+
         def products(s):
             b, t = divmod(s, PACK)
             rows = slice(P * t, P * (t + 1))
-            h[s] = ring.tile([P, S], F32, name="h", tag="h", bufs=6, align_bytes=64)
+            if s not in h:
+                new_h(s)
             for c in range(S // BANK):
-                cols = slice(BANK * c, BANK * (c + 1))
-                second = psum.tile([P, BANK], F32, name="second", tag="second", bufs=3)
+                width = plain_width(s, c)
+                if width == 0:
+                    continue
+                cols = slice(BANK * c, BANK * c + width)
+                second = psum.tile([P, width], F32, name="second", tag="second", bufs=3)
                 nc.tensor.matmul_mx(
                     out=second[:],
                     lhsT=w4_w[:, 2 * P * s : 2 * P * (s + 1)].bitcast(FP4X4),
                     lhsT_scale=w4_s[:, P * s : P * (s + 1)],
-                    rhs=v_w[c][:].bitcast(FP8X4),
+                    rhs=v_w[c][:, :width].bitcast(FP8X4),
                     rhs_scale=v_s[:, cols],
                     start=True,
                     stop=True,
                 )
-                scaled = ring.tile([P, BANK], F32, name="scaled", tag="scaled", bufs=6, align_bytes=64)
+                scaled = reused("scaled", [P, width], F32, f"staged{s % 2}{c}")
                 nc.scalar.activation(out=scaled[:], in_=second[:], func=ACT.Copy, scale=gain_abs[:, s : s + 1])
-                first = psum.tile([P, BANK], F32, name="first", tag="first", bufs=5)
+                first = psum.tile([P, width], F32, name="first", tag="first", bufs=5)
                 nc.tensor.matmul_mx(
                     out=first[:],
                     lhsT=w1_w[b][:, rows].bitcast(FP8X4),
                     lhsT_scale=w1_s[b][:, rows],
-                    rhs=v_w[c][:].bitcast(FP8X4),
+                    rhs=v_w[c][:, :width].bitcast(FP8X4),
                     rhs_scale=v_s[:, cols],
                     start=True,
                     stop=True,
                 )
-                readings[s, c] = (first, scaled)
+                readings[s, c] = (first, scaled, cols)
 
         def larger(s, cs):
             for c in cs:
-                first, scaled = readings[s, c]
+                if (s, c) not in readings:
+                    continue
+                first, scaled, cols = readings[s, c]
                 nc.vector.scalar_tensor_tensor(
-                    out=h[s][:, BANK * c : BANK * (c + 1)],
+                    out=h[s][:, cols],
                     in0=first[:],
-                    scalar=gain_abs[:, s : s + 1],
+                    scalar=gain_w1[:, s : s + 1],
                     in1=scaled[:],
                     op0=ALU.mult,
                     op1=ALU.max,
                 )
 
-        def seed_side(s, m0, width, buffer="xa", bufs=4):
-            xa = ring.tile([P, width], F32, name="xa", tag=buffer, bufs=bufs, align_bytes=64)
+        turned = {}
+
+        def turned_products(block):
+            j0 = S - TURNED * P + P * block
+            c, lo = divmod(j0, BANK)
+            table = dict(lhsT=v_w[c][:, lo : lo + P].bitcast(FP8X4), lhsT_scale=v_s[:, j0 : j0 + P])
+            minus_first = dict(rhs=w1_w[1][:].bitcast(FP8X4), rhs_scale=w1_s[1][:])
+            diff = psum.tile([P, BANK], F32, name="diff", tag="second", bufs=3)
+            nc.tensor.matmul_mx(
+                out=diff[:], rhs=w4_w[:, H:].bitcast(FP4X4), rhs_scale=w4_s[:, BANK:], start=True, stop=False, **table
+            )
+            nc.tensor.matmul_mx(out=diff[:], start=False, stop=True, **table, **minus_first)
+            excess = reused("excess", [P, BANK], F32, f"turned{2 * block}")
+            nc.scalar.activation(out=excess[:], in_=diff[:], func=ACT.Relu)
+            alone = psum.tile([P, BANK], F32, name="alone", tag="second", bufs=3)
+            nc.tensor.matmul_mx(out=alone[:], start=True, stop=True, **table, **minus_first)
+            base = reused("base", [P, BANK], F32, f"turned{2 * block + 1}")
+            nc.scalar.activation(out=base[:], in_=alone[:], func=ACT.Copy, scale=-1.0)
+            turned[block] = (base, excess)
+
+        def turn_back(s):
+            t = s - PACK
+            for first_block in range(0, TURNED, BANK // P):
+                blocks = range(first_block, min(TURNED, first_block + BANK // P))
+                bank = psum.tile([P, len(blocks) * P], F32, name="back", tag="second", bufs=3)
+                for i, block in enumerate(blocks):
+                    for k, part in enumerate(turned[block]):
+                        nc.tensor.matmul(
+                            bank[:, P * i : P * (i + 1)],
+                            lhsT=part[:, P * t : P * (t + 1)],
+                            rhs=identity[:],
+                            is_transpose=True,
+                            start=(k == 0),
+                            stop=(k == 1),
+                        )
+                j0 = S - TURNED * P + P * first_block
+                nc.scalar.activation(
+                    out=h[s][:, j0 : j0 + len(blocks) * P], in_=bank[:], func=ACT.Copy, scale=gain_abs[:, s : s + 1]
+                )
+
+        def seed_side(s, m0, xa):
+            width = xa.shape[1]
             cols = slice(m0 // PER_COL, (m0 + width) // PER_COL)
             nc.vector.tensor_tensor(
                 out=xa[:], in0=h[s][:].indirect(seeds[:, cols]), in1=weight[:, m0 : m0 + width], op=ALU.mult
             )
-            return xa
 
-        def pollen_side(s, m0, width, xa, dst):
-            cols = slice(m0 // PER_COL, (m0 + width) // PER_COL)
+        def pollen_side(s, m0, xa, dst):
+            cols = slice(m0 // PER_COL, (m0 + xa.shape[1]) // PER_COL)
             nc.vector.tensor_tensor(out=dst, in0=h[s][:].indirect(pollen[:, cols]), in1=xa[:], op=ALU.mult)
 
         x_w = [held(f"x_w{b}", [P, M], U32) for b in range(PASSES)]
         x_s = [held(f"x_s{b}", [P, M], U8) for b in range(PASSES)]
 
-        def round_x(src, width, engine_copy, tag="x_bf", bufs=2):
-            x_bf = ring.tile([P, PACK * width], BF16, name="x_bf", tag=tag, bufs=bufs, align_bytes=64)
+        def round_x(src, engine_copy, buffer):
+            x_bf = reused("x_bf", [P, PACK * src.shape[2]], BF16, buffer)
             interleave(x_bf[:], src, engine_copy)
             return x_bf
 
-        def quantise_x(b, m0, width, x_bf):
-            cols = slice(m0, m0 + width)
+        def quantise_x(b, m0, x_bf):
+            cols = slice(m0, m0 + x_bf.shape[1] // PACK)
             nc.vector.quantize_mx(out=x_w[b][:, cols].bitcast(FP8X4), scales=x_s[b][:, cols], in_=x_bf[:])
 
         out_rows = out.rearrange("(c p) m -> p c m", p=P)
+        starts = [sum(CHUNKS[:i]) for i in range(len(CHUNKS))]
+        banks = {}
 
-        def score_banks(width, tag, bufs):
-            per_bank = min(N_TILES, BANK // width)
-            accs = []
-            for c0 in range(0, N_TILES, per_bank):
-                count = min(per_bank, N_TILES - c0)
-                bank = psum.tile([P, count, width], F32, name="acc", tag=tag, bufs=bufs)
-                accs.append((bank, c0, count))
-            return accs
-
-        def score_pass(b, m0, width, accs):
-            cols = slice(m0, m0 + width)
-            for bank, c0, count in accs:
-                for i in range(count):
-                    ns = slice(P * (c0 + i), P * (c0 + i + 1))
+        def score_pass(b, i):
+            width = CHUNKS[i]
+            cols = slice(starts[i], starts[i] + width)
+            if b == 0:
+                per_bank = min(N_TILES, BANK // width)
+                tag, bufs = ("first", 5) if width > P else ("second", 3)
+                banks[i] = []
+                for c0 in range(0, N_TILES, per_bank):
+                    count = min(per_bank, N_TILES - c0)
+                    banks[i].append((psum.tile([P, count, width], F32, name="acc", tag=tag, bufs=bufs), c0, count))
+            for bank, c0, count in banks[i]:
+                for k in range(count):
+                    ns = slice(P * (c0 + k), P * (c0 + k + 1))
                     nc.tensor.matmul_mx(
-                        out=bank[:, i, :],
+                        out=bank[:, k, :],
                         lhsT=w2_w[b][:, ns].bitcast(FP8X4),
                         lhsT_scale=w2_s[b][:, ns],
                         rhs=x_w[b][:, cols].bitcast(FP8X4),
                         rhs_scale=x_s[b][:, cols],
-                        start=(b == 0 and i == 0),
-                        stop=(b == PASSES - 1 and i == count - 1),
+                        start=(b == 0 and k == 0),
+                        stop=(b == PASSES - 1 and k == count - 1),
                     )
 
-        def store_scores(m0, width, accs, on_vector):
-            res = held(f"res{m0}", [P, N_TILES, width], F32)
-            for bank, c0, count in accs:
+        def store(i, on_vector):
+            width = CHUNKS[i]
+            res = reused("res", [P, N_TILES, width], F32, ("w1_raw0", "w1_raw1", "weight_a", "weight_b")[i])
+            for bank, c0, count in banks[i]:
                 if on_vector:
                     nc.vector.tensor_tensor(
                         out=res[:, c0 : c0 + count, :],
@@ -262,102 +315,89 @@ def tile_list_testcross_heterosis_scores_kernel(
                         op=ALU.add,
                     )
                 else:
-                    for i in range(count):
-                        c = c0 + i
+                    for k in range(count):
+                        c = c0 + k
                         nc.scalar.activation(
-                            out=res[:, c, :], in_=bank[:, i, :], func=ACT.Identity, bias=tester_col[:, c : c + 1], scale=1.0
+                            out=res[:, c, :], in_=bank[:, k, :], func=ACT.Identity, bias=tester_col[:, c : c + 1], scale=1.0
                         )
-            nc.sync.dma_start(out=out_rows[:, :, m0 : m0 + width], in_=res[:])
+            nc.sync.dma_start(out=out_rows[:, :, starts[i] : starts[i] + width], in_=res[:])
 
         round_w1(0)
-        quantise_w1(0, 0, 4)
+        nc.scalar.activation(out=gain_abs[:], in_=gain_raw[:].rearrange("p b t -> p (b t)"), func=ACT.Abs)
+        nc.scalar.activation(out=gain_w1[:, :PACK], in_=gain_abs[:, :PACK], func=ACT.Copy)
+        nc.scalar.activation(out=gain_w1[:, PACK:], in_=gain_abs[:, PACK:], func=ACT.Copy, scale=-1.0)
+        quantise_w1(0)
         pick_words(3)
         weight = reused("weight", [P, M], F32, "table")
         nc.gpsimd.tensor_tensor(out=weight[:], in0=weight_a[:], in1=weight_b[:], op=ALU.mult)
         products(0)
-        larger(0, range(4))
         products(1)
         round_w1(1)
-        larger(1, range(4))
+        larger(0, range(4))
+        quantise_w1(1)
 
         x0 = held("x0", [P, PACK, M], F32)
-        for s in range(PACK):
-            products(s + 2)
-            if s == 0:
-                quantise_w1(1, 0, 4)
-            if s in (1, 2):
-                interleave(w2_bf[s - 1][:], w2_raw[s - 1][:], nc.scalar.copy)
-            xa = seed_side(s, 0, M)
-            larger(s + 2, (0, 1))
-            pollen_side(s, 0, M, xa, x0[:, s, :])
-            larger(s + 2, (2, 3))
+        x1 = {0: held("x1_0", [P, PACK, CHUNKS[0]], F32)}
+        x0_bf = []
+        for s in range(SLICES):
+            b, t = divmod(s, PACK)
+            half = (M, CHUNKS[0])[b] // 2
+            dst = (x0, x1[0])[b]
+            if s + 2 < SLICES:
+                products(s + 2)
+            for block in TURNED_AT.get(s, ()):
+                turned_products(block)
+            if PACK <= s + 1 < SLICES:
+                turn_back(s + 1)
+            if s in (2, 3):
+                interleave(w2_bf[s - 2][:], w2_raw[s - 2][:], nc.scalar.copy)
+            if s in (4, 5):
+                x0_bf.append(round_x(x0[:, :, BANK * (s - 4) : BANK * (s - 3)], nc.scalar.copy, f"w1_raw{s - 2}"))
+            larger(s + 1, (0, 1))
+            xas = [reused("xa", [P, half], F32, f"staged{(s + 1) % 2}{i}") for i in range(2)]
+            for i in range(2):
+                seed_side(s, half * i, xas[i])
+            larger(s + 1, (2, 3))
+            for i in range(2):
+                pollen_side(s, half * i, xas[i], dst[:, t, half * i : half * (i + 1)])
+            if s in (4, 5):
+                quantise_w2(s - 4)
+            if s in (6, 7):
+                quantise_x(0, BANK * (s - 6), x0_bf[s - 6])
 
-        width = LAST_PASS_CHUNKS[0]
-        x1 = {0: held("x1_0", [P, PACK, width], F32)}
-        products(6)
-        x0_bf = [round_x(x0[:, :, BANK * i : BANK * (i + 1)], BANK, nc.scalar.copy) for i in range(2)]
-        xa4 = seed_side(4, 0, width)
-        xa5 = seed_side(5, 0, width)
-        larger(6, (0, 1))
-        pollen_side(4, 0, width, xa4, x1[0][:, 0, :])
-        larger(6, (2, 3))
-        products(7)
-        pollen_side(5, 0, width, xa5, x1[0][:, 1, :])
-        xa6 = seed_side(6, 0, width)
-        quantise_w2(0)
-        quantise_w2(1)
-        pollen_side(6, 0, width, xa6, x1[0][:, 2, :])
-        larger(7, range(4))
-        quantise_x(0, 0, BANK, x0_bf[0])
-        xa7 = seed_side(7, 0, width)
-        quantise_x(0, BANK, BANK, x0_bf[1])
-        pollen_side(7, 0, width, xa7, x1[0][:, 3, :])
+        for i in range(len(CHUNKS)):
+            score_pass(0, i)
 
-        starts = [sum(LAST_PASS_CHUNKS[:i]) for i in range(len(LAST_PASS_CHUNKS))]
-        banks = []
-        for m0, w in zip(starts, LAST_PASS_CHUNKS):
-            banks.append(score_banks(w, "first", 5) if w > P else score_banks(w, "second", 3))
-            score_pass(0, m0, w, banks[-1])
+        def crosses(i, ts, buffers):
+            xas = [reused("xa", [P, CHUNKS[i]], F32, buffer) for buffer in buffers]
+            for t, xa in zip(ts, xas):
+                seed_side(PACK + t, starts[i], xa)
+            for t, xa in zip(ts, xas):
+                pollen_side(PACK + t, starts[i], xa, x1[i][:, t, :])
 
-        def finish(i, x_bf):
-            quantise_x(1, starts[i], LAST_PASS_CHUNKS[i], x_bf)
-            score_pass(1, starts[i], LAST_PASS_CHUNKS[i], banks[i])
-
-        def store(i, on_vector=False):
-            store_scores(starts[i], LAST_PASS_CHUNKS[i], banks[i], on_vector)
-
-        def seeds_of(i, ts, first_buffer=None):
-            xas = {}
-            for t in ts:
-                if first_buffer and t == ts[0]:
-                    xas[t] = seed_side(PACK + t, starts[i], LAST_PASS_CHUNKS[i], first_buffer, 1)
-                else:
-                    xas[t] = seed_side(PACK + t, starts[i], LAST_PASS_CHUNKS[i])
-            return xas
-
-        def pollen_of(i, xas):
-            for t in xas:
-                pollen_side(PACK + t, starts[i], LAST_PASS_CHUNKS[i], xas[t], x1[i][:, t, :])
-
-        bf0 = round_x(x1[0][:], LAST_PASS_CHUNKS[0], nc.scalar.copy, "tail0", 1)
-        x1[1] = held("x1_1", [P, PACK, LAST_PASS_CHUNKS[1]], F32)
-        pollen_of(1, seeds_of(1, (0, 1)))
-        xas = seeds_of(1, (2,))
-        finish(0, bf0)
-        xas[3] = seeds_of(1, (3,), "tail0")[3]
-        pollen_of(1, xas)
-        store(0)
-        bf1 = round_x(x1[1][:], LAST_PASS_CHUNKS[1], nc.scalar.copy, "tail1", 1)
-        x1[2] = held("x1_2", [P, PACK, LAST_PASS_CHUNKS[2]], F32)
-        pollen_of(2, seeds_of(2, (0, 1, 2, 3)))
-        bf2 = round_x(x1[2][:], LAST_PASS_CHUNKS[2], nc.scalar.copy, "tail2", 1)
-        finish(1, bf1)
-        xas = seeds_of(3, (0, 1, 2, 3), "tail1")
-        store(1)
-        finish(2, bf2)
-        x1[3] = reused("x1_3", [P, PACK, LAST_PASS_CHUNKS[3]], F32, "tail2")
-        pollen_of(3, xas)
-        store(2)
-        bf3 = round_x(x1[3][:], LAST_PASS_CHUNKS[3], nc.vector.tensor_copy, "tail3", 1)
-        finish(3, bf3)
+        for i in range(1, len(CHUNKS)):
+            x1[i] = held(f"x1_{i}", [P, PACK, CHUNKS[i]], F32)
+        half = CHUNKS[0] // 2
+        bf0 = [round_x(x1[0][:, :, half * i : half * (i + 1)], nc.scalar.copy, f"tail0{i}") for i in range(2)]
+        crosses(1, (0, 1), ("staged00", "staged01"))
+        for i in range(2):
+            quantise_x(1, half * i, bf0[i])
+        score_pass(1, 0)
+        crosses(1, (2, 3), ("tail00", "tail01"))
+        bf1 = round_x(x1[1][:], nc.scalar.copy, "tail1")
+        store(0, False)
+        crosses(2, (0, 1), ("tail00", "tail01"))
+        crosses(2, (2, 3), ("tail00", "tail01"))
+        bf2 = round_x(x1[2][:], nc.scalar.copy, "tail2")
+        quantise_x(1, starts[1], bf1)
+        score_pass(1, 1)
+        crosses(3, (0, 1), ("tail1", "tail01"))
+        store(1, False)
+        quantise_x(1, starts[2], bf2)
+        score_pass(1, 2)
+        crosses(3, (2, 3), ("tail2", "tail1"))
+        store(2, False)
+        bf3 = round_x(x1[3][:], nc.vector.tensor_copy, "tail3")
+        quantise_x(1, starts[3], bf3)
+        score_pass(1, 3)
         store(3, True)

@@ -24,7 +24,7 @@ PASSES = H // (P * PACK)
 SLICES = H // P
 PER_COL = 16
 N_TILES = N // P
-W1_PIECE = 256
+SCALE_ROWS = K // 32
 CHUNKS = (512, 256, 128, 128)
 TURNED = 7
 TURNED_AT = {0: (0, 1), 1: (2, 3, 4), 2: (5, 6)}
@@ -56,21 +56,23 @@ def tile_list_testcross_heterosis_scores_kernel(
         identity = held("identity", [P, P], F32)
         make_identity(nc, identity[:])
 
+        v_s = held("v_s", [P, S], U8)
+        nc.vector.memset(tab_s[: P - SCALE_ROWS, :].bitcast(I32), 0)
+        nc.vector.memset(v_s[:].bitcast(I32), 0)
+
         nc.sync.dma_start(out=lines[:], in_=offs)
-        for q in range(4):
-            nc.sync.dma_start(
-                out=tab_s[32 * q : 32 * (q + 1), :].bitcast(I32),
-                in_=tab_scales[0, 4 * q : 4 * q + 4, :].bitcast(I32).partition_broadcast(8),
-            )
+        nc.sync.dma_start(out=tab_s[P - SCALE_ROWS :, :].bitcast(I32), in_=tab_scales[0].bitcast(I32))
+        gain_raw = held("gain_raw", [P, PASSES, PACK], F32)
+        nc.sync.dma_start(out=gain_raw[:], in_=gain.rearrange("(b p t) -> p b t", b=PASSES, t=PACK))
+        nc.sync.dma_start(out=seeds[:], in_=offs2)
+        nc.sync.dma_start(out=pollen[:], in_=offs3)
         nc.sync.dma_start(out=tab_w[:].bitcast(I32), in_=tab_words[0].rearrange("p t i -> p (t i)").bitcast(I32))
 
         w1_rows = w1.rearrange("(p j) r -> p j r", j=PACK)
-        w1_raw = [reused("w1_raw", [P, PACK, W1_PIECE], F32, f"w1_raw{piece}") for piece in range(H // W1_PIECE)]
+        w1_raw = [reused("w1_raw", [P, PACK, BANK], F32, f"w1_raw{b}") for b in range(PASSES)]
 
         def load_w1(b):
-            for piece in (2 * b, 2 * b + 1):
-                cols = slice(W1_PIECE * piece, W1_PIECE * (piece + 1))
-                nc.sync.dma_start(out=w1_raw[piece][:], in_=w1_rows[:, :, cols])
+            nc.sync.dma_start(out=w1_raw[b][:], in_=w1_rows[:, :, BANK * b : BANK * (b + 1)])
 
         load_w1(0)
         nc.sync.dma_start(out=w4_w_raw[:].bitcast(I32), in_=w4_words[0].bitcast(I32))
@@ -78,14 +80,17 @@ def tile_list_testcross_heterosis_scores_kernel(
             nc.sync.dma_start(
                 out=w4_s_raw[32 * q : 32 * q + 4, :].bitcast(I32), in_=w4_scales[0, 4 * q : 4 * q + 4, :].bitcast(I32)
             )
-        gain_raw = held("gain_raw", [P, PASSES, PACK], F32)
-        nc.sync.dma_start(out=gain_raw[:], in_=gain.rearrange("(b p t) -> p b t", b=PASSES, t=PACK))
+
+        picked_s = reused("picked_s", [P, S], U8, "tail2")
+        nc.vector.tensor_copy(out=picked_s[:], in_=tab_s[:].indirect(lines[:]))
+        for q in range(4):
+            row = P - SCALE_ROWS + 4 * q
+            nc.sync.dma_start(out=v_s[32 * q : 32 * q + 4, :].bitcast(I32), in_=picked_s[row : row + 4, :].bitcast(I32))
+
         weight_a = reused("weight_a", [P, M], F32, "weight_a")
         weight_b = reused("weight_b", [P, M], F32, "weight_b")
         nc.sync.dma_start(out=weight_a[:], in_=wga)
         nc.sync.dma_start(out=weight_b[:], in_=wgb)
-        nc.sync.dma_start(out=seeds[:], in_=offs2)
-        nc.sync.dma_start(out=pollen[:], in_=offs3)
         load_w1(1)
         w2_raw = []
         for b in range(PASSES):
@@ -96,8 +101,6 @@ def tile_list_testcross_heterosis_scores_kernel(
         with nc.allow_non_contiguous_dma(reason="one value of tester for each partition"):
             nc.sync.dma_start(out=tester_col[:], in_=tester.rearrange("(c p) -> p c", p=P))
 
-        v_s = held("v_s", [P, S], U8)
-        nc.vector.tensor_copy(out=v_s[:], in_=tab_s[:].indirect(lines[:]))
         v_w = []
 
         def pick_words(c):
@@ -128,14 +131,12 @@ def tile_list_testcross_heterosis_scores_kernel(
         w1_bf = [reused("w1_bf", [P, PACK, P, PACK], BF16, buffer) for buffer in ("picked3", "w1_bf")]
 
         def round_w1(b):
-            for half in range(2):
-                ms = slice(P // 2 * half, P // 2 * (half + 1))
-                nc.scalar.activation(
-                    out=w1_bf[b][:, :, ms, :].rearrange("p t m j -> p m t j"),
-                    in_=w1_raw[2 * b + half][:].rearrange("p j (m t) -> p m t j", t=PACK),
-                    func=ACT.Copy,
-                    scale=(1.0, -1.0)[b],
-                )
+            nc.scalar.activation(
+                out=w1_bf[b][:].rearrange("p t m j -> p m t j"),
+                in_=w1_raw[b][:].rearrange("p j (m t) -> p m t j", t=PACK),
+                func=ACT.Copy,
+                scale=(1.0, -1.0)[b],
+            )
 
         def quantise_w1(b):
             nc.vector.quantize_mx(
@@ -352,7 +353,7 @@ def tile_list_testcross_heterosis_scores_kernel(
             if s in (2, 3):
                 interleave(w2_bf[s - 2][:], w2_raw[s - 2][:], nc.scalar.copy)
             if s in (4, 5):
-                x0_bf.append(round_x(x0[:, :, BANK * (s - 4) : BANK * (s - 3)], nc.scalar.copy, f"w1_raw{s - 2}"))
+                x0_bf.append(round_x(x0[:, :, BANK * (s - 4) : BANK * (s - 3)], nc.scalar.copy, ("weight_a", "weight_b")[s - 4]))
             larger(s + 1, (0, 1))
             xas = [reused("xa", [P, half], F32, f"staged{(s + 1) % 2}{i}") for i in range(2)]
             for i in range(2):

from contextlib import ExitStack

import concourse.mybir as mybir
from concourse.masks import make_identity

K, H, N, T, S, M = 512, 1024, 384, 4096, 2048, 1024
FLOPS = 2 * (2 * K * H * S + H * N * M)

F32 = mybir.dt.float32
BF16 = mybir.dt.bfloat16
I32 = mybir.dt.int32
U32 = mybir.dt.uint32
U16 = mybir.dt.uint16
U8 = mybir.dt.uint8
FP8X4 = mybir.dt.float8_e4m3fn_x4
FP4X4 = mybir.dt.float4_e2m1fn_x4
ALU = mybir.AluOpType
ACT = mybir.ActivationFunctionType

P = 128
PACK = 4
BANK = 512
PASSES = H // (P * PACK)
SLICES = H // P
PER_COL = 16
N_TILES = N // P
SCALE_ROWS = K // 32
CHUNKS = (512, 256, 128, 128)
TURNED = 7
TURNED_AT = {0: (0, 1), 1: (2, 3, 4), 2: (5, 6)}


def tile_list_testcross_heterosis_scores_kernel(
    tc, tab_words, tab_scales, offs, offs2, offs3, w1, w4_words, w4_scales, gain, wga, wgb, w2, tester, out
):
    nc = tc.nc
    with ExitStack() as ctx:
        keep = ctx.enter_context(tc.tile_pool(name="keep", bufs=1))
        ring = ctx.enter_context(tc.tile_pool(name="ring", bufs=1))
        psum = ctx.enter_context(tc.psum_pool(name="psum", bufs=1))

        def held(name, shape, dtype):
            return keep.tile(shape, dtype, name=name, align_bytes=64)

        def reused(name, shape, dtype, buffer):
            return ring.tile(shape, dtype, name=name, tag=buffer, bufs=1, align_bytes=64)

        lines = held("lines", [P, S // PER_COL], U16)
        seeds = held("seeds", [P, M // PER_COL], U16)
        pollen = held("pollen", [P, M // PER_COL], U16)
        tab_w = reused("tab_w", [P, T], U32, "table")
        tab_s = held("tab_s", [P, T], U8)
        w4_w_raw = reused("w4_w_raw", [P, 2 * H], U8, "tail1")
        w4_s_raw = held("w4_s_raw", [P, H], U8)
        nc.gpsimd.memset(w4_s_raw[:].bitcast(I32), 0)
        identity = held("identity", [P, P], F32)
        make_identity(nc, identity[:])

        v_s = held("v_s", [P, S], U8)
        nc.vector.memset(tab_s[: P - SCALE_ROWS, :].bitcast(I32), 0)
        nc.vector.memset(v_s[:].bitcast(I32), 0)

        nc.sync.dma_start(out=lines[:], in_=offs)
        nc.sync.dma_start(out=tab_s[P - SCALE_ROWS :, :].bitcast(I32), in_=tab_scales[0].bitcast(I32))
        gain_raw = held("gain_raw", [P, PASSES, PACK], F32)
        nc.sync.dma_start(out=gain_raw[:], in_=gain.rearrange("(b p t) -> p b t", b=PASSES, t=PACK))
        nc.sync.dma_start(out=seeds[:], in_=offs2)
        nc.sync.dma_start(out=pollen[:], in_=offs3)
        nc.sync.dma_start(out=tab_w[:].bitcast(I32), in_=tab_words[0].rearrange("p t i -> p (t i)").bitcast(I32))

        w1_rows = w1.rearrange("(p j) r -> p j r", j=PACK)
        w1_raw = [reused("w1_raw", [P, PACK, BANK], F32, f"w1_raw{b}") for b in range(PASSES)]

        def load_w1(b):
            nc.sync.dma_start(out=w1_raw[b][:], in_=w1_rows[:, :, BANK * b : BANK * (b + 1)])

        load_w1(0)
        nc.sync.dma_start(out=w4_w_raw[:].bitcast(I32), in_=w4_words[0].bitcast(I32))
        for q in range(4):
            nc.sync.dma_start(
                out=w4_s_raw[32 * q : 32 * q + 4, :].bitcast(I32), in_=w4_scales[0, 4 * q : 4 * q + 4, :].bitcast(I32)
            )

        picked_s = reused("picked_s", [P, S], U8, "tail2")
        nc.vector.tensor_copy(out=picked_s[:], in_=tab_s[:].indirect(lines[:]))
        for q in range(4):
            row = P - SCALE_ROWS + 4 * q
            nc.sync.dma_start(out=v_s[32 * q : 32 * q + 4, :].bitcast(I32), in_=picked_s[row : row + 4, :].bitcast(I32))

        weight_a = reused("weight_a", [P, M], F32, "weight_a")
        weight_b = reused("weight_b", [P, M], F32, "weight_b")
        nc.sync.dma_start(out=weight_a[:], in_=wga)
        nc.sync.dma_start(out=weight_b[:], in_=wgb)
        load_w1(1)
        w2_raw = []
        for b in range(PASSES):
            raw = held(f"w2_raw{b}", [P, PACK, N], F32)
            nc.sync.dma_start(out=raw[:], in_=w2[BANK * b : BANK * (b + 1), :].rearrange("(p j) n -> p j n", j=PACK))
            w2_raw.append(raw)
        tester_col = held("tester_col", [P, N_TILES], F32)
        with nc.allow_non_contiguous_dma(reason="one value of tester for each partition"):
            nc.sync.dma_start(out=tester_col[:], in_=tester.rearrange("(c p) -> p c", p=P))

        v_w = []

        def pick_words(c):
            picked = reused("v_w", [P, BANK], U32, f"picked{c}")
            cols = slice(c * BANK // PER_COL, (c + 1) * BANK // PER_COL)
            nc.vector.tensor_copy(out=picked[:], in_=tab_w[:].indirect(lines[:, cols]))
            v_w.append(picked)

        pick_words(0)
        pick_words(1)
        pick_words(2)
        w4_w = held("w4_w", [P, 2 * H], U8)
        w4_s = held("w4_s", [P, H], U8)
        nc.vector.tensor_copy(
            out=w4_w[:].bitcast(U16).rearrange("p (b t m) -> p b t m", b=PASSES, t=PACK),
            in_=w4_w_raw[:].bitcast(U16).rearrange("p (b m t) -> p b t m", b=PASSES, t=PACK),
        )
        nc.vector.tensor_copy(
            out=w4_s[:].rearrange("p (b t m) -> p b t m", b=PASSES, t=PACK),
            in_=w4_s_raw[:].rearrange("p (b m t) -> p b t m", b=PASSES, t=PACK),
        )

        gain_abs = held("gain_abs", [P, SLICES], F32)
        gain_w1 = held("gain_w1", [P, SLICES], F32)

        w1_w = [held(f"w1_w{b}", [P, BANK], U32) for b in range(PASSES)]
        w1_s = [held(f"w1_s{b}", [P, BANK], U8) for b in range(PASSES)]
        w1_bf = [reused("w1_bf", [P, PACK, P, PACK], BF16, buffer) for buffer in ("picked3", "w1_bf")]

        def round_w1(b):
            nc.scalar.activation(
                out=w1_bf[b][:].rearrange("p t m j -> p m t j"),
                in_=w1_raw[b][:].rearrange("p j (m t) -> p m t j", t=PACK),
                func=ACT.Copy,
                scale=(1.0, -1.0)[b],
            )

        def quantise_w1(b):
            nc.vector.quantize_mx(
                out=w1_w[b][:].bitcast(FP8X4), scales=w1_s[b][:], in_=w1_bf[b][:].rearrange("p t m j -> p (t m j)")
            )

        def interleave(dst, src, engine_copy):
            engine_copy(
                out=dst.rearrange("p (c i t) -> p c t i", i=4, t=PACK),
                in_=src.rearrange("p t (c i) -> p c t i", i=4),
            )

        w2_w = [held(f"w2_w{b}", [P, N], U32) for b in range(PASSES)]
        w2_s = [held(f"w2_s{b}", [P, N], U8) for b in range(PASSES)]
        w2_bf = [held(f"w2_bf{b}", [P, N * PACK], BF16) for b in range(PASSES)]

        def quantise_w2(b):
            nc.vector.quantize_mx(out=w2_w[b][:].bitcast(FP8X4), scales=w2_s[b][:], in_=w2_bf[b][:])

        h = {}
        readings = {}

        def plain_width(s, c):
            plain = S - (TURNED * P if s >= PACK else 0)
            return max(0, min(BANK, plain - BANK * c))

        def new_h(s):
            h[s] = ring.tile([P, S], F32, name="h", tag="h", bufs=6, align_bytes=64)

        def products(s):
            b, t = divmod(s, PACK)
            rows = slice(P * t, P * (t + 1))
            if s not in h:
                new_h(s)
            for c in range(S // BANK):
                width = plain_width(s, c)
                if width == 0:
                    continue
                cols = slice(BANK * c, BANK * c + width)
                second = psum.tile([P, width], F32, name="second", tag="second", bufs=3)
                nc.tensor.matmul_mx(
                    out=second[:],
                    lhsT=w4_w[:, 2 * P * s : 2 * P * (s + 1)].bitcast(FP4X4),
                    lhsT_scale=w4_s[:, P * s : P * (s + 1)],
                    rhs=v_w[c][:, :width].bitcast(FP8X4),
                    rhs_scale=v_s[:, cols],
                    start=True,
                    stop=True,
                )
                scaled = reused("scaled", [P, width], F32, f"staged{s % 2}{c}")
                nc.scalar.activation(out=scaled[:], in_=second[:], func=ACT.Copy, scale=gain_abs[:, s : s + 1])
                first = psum.tile([P, width], F32, name="first", tag="first", bufs=5)
                nc.tensor.matmul_mx(
                    out=first[:],
                    lhsT=w1_w[b][:, rows].bitcast(FP8X4),
                    lhsT_scale=w1_s[b][:, rows],
                    rhs=v_w[c][:, :width].bitcast(FP8X4),
                    rhs_scale=v_s[:, cols],
                    start=True,
                    stop=True,
                )
                readings[s, c] = (first, scaled, cols)

        def larger(s, cs):
            for c in cs:
                if (s, c) not in readings:
                    continue
                first, scaled, cols = readings[s, c]
                nc.vector.scalar_tensor_tensor(
                    out=h[s][:, cols],
                    in0=first[:],
                    scalar=gain_w1[:, s : s + 1],
                    in1=scaled[:],
                    op0=ALU.mult,
                    op1=ALU.max,
                )

        turned = {}

        def turned_products(block):
            j0 = S - TURNED * P + P * block
            c, lo = divmod(j0, BANK)
            table = dict(lhsT=v_w[c][:, lo : lo + P].bitcast(FP8X4), lhsT_scale=v_s[:, j0 : j0 + P])
            minus_first = dict(rhs=w1_w[1][:].bitcast(FP8X4), rhs_scale=w1_s[1][:])
            diff = psum.tile([P, BANK], F32, name="diff", tag="second", bufs=3)
            nc.tensor.matmul_mx(
                out=diff[:], rhs=w4_w[:, H:].bitcast(FP4X4), rhs_scale=w4_s[:, BANK:], start=True, stop=False, **table
            )
            nc.tensor.matmul_mx(out=diff[:], start=False, stop=True, **table, **minus_first)
            excess = reused("excess", [P, BANK], F32, f"turned{2 * block}")
            nc.scalar.activation(out=excess[:], in_=diff[:], func=ACT.Relu)
            alone = psum.tile([P, BANK], F32, name="alone", tag="second", bufs=3)
            nc.tensor.matmul_mx(out=alone[:], start=True, stop=True, **table, **minus_first)
            base = reused("base", [P, BANK], F32, f"turned{2 * block + 1}")
            nc.scalar.activation(out=base[:], in_=alone[:], func=ACT.Copy, scale=-1.0)
            turned[block] = (base, excess)

        def turn_back(s):
            t = s - PACK
            for first_block in range(0, TURNED, BANK // P):
                blocks = range(first_block, min(TURNED, first_block + BANK // P))
                bank = psum.tile([P, len(blocks) * P], F32, name="back", tag="second", bufs=3)
                for i, block in enumerate(blocks):
                    for k, part in enumerate(turned[block]):
                        nc.tensor.matmul(
                            bank[:, P * i : P * (i + 1)],
                            lhsT=part[:, P * t : P * (t + 1)],
                            rhs=identity[:],
                            is_transpose=True,
                            start=(k == 0),
                            stop=(k == 1),
                        )
                j0 = S - TURNED * P + P * first_block
                nc.scalar.activation(
                    out=h[s][:, j0 : j0 + len(blocks) * P], in_=bank[:], func=ACT.Copy, scale=gain_abs[:, s : s + 1]
                )

        def seed_side(s, m0, xa):
            width = xa.shape[1]
            cols = slice(m0 // PER_COL, (m0 + width) // PER_COL)
            nc.vector.tensor_tensor(
                out=xa[:], in0=h[s][:].indirect(seeds[:, cols]), in1=weight[:, m0 : m0 + width], op=ALU.mult
            )

        def pollen_side(s, m0, xa, dst):
            cols = slice(m0 // PER_COL, (m0 + xa.shape[1]) // PER_COL)
            nc.vector.tensor_tensor(out=dst, in0=h[s][:].indirect(pollen[:, cols]), in1=xa[:], op=ALU.mult)

        x_w = [held(f"x_w{b}", [P, M], U32) for b in range(PASSES)]
        x_s = [held(f"x_s{b}", [P, M], U8) for b in range(PASSES)]

        def round_x(src, engine_copy, buffer):
            x_bf = reused("x_bf", [P, PACK * src.shape[2]], BF16, buffer)
            interleave(x_bf[:], src, engine_copy)
            return x_bf

        def quantise_x(b, m0, x_bf):
            cols = slice(m0, m0 + x_bf.shape[1] // PACK)
            nc.vector.quantize_mx(out=x_w[b][:, cols].bitcast(FP8X4), scales=x_s[b][:, cols], in_=x_bf[:])

        out_rows = out.rearrange("(c p) m -> p c m", p=P)
        starts = [sum(CHUNKS[:i]) for i in range(len(CHUNKS))]
        banks = {}

        def score_pass(b, i):
            width = CHUNKS[i]
            cols = slice(starts[i], starts[i] + width)
            if b == 0:
                per_bank = min(N_TILES, BANK // width)
                tag, bufs = ("first", 5) if width > P else ("second", 3)
                banks[i] = []
                for c0 in range(0, N_TILES, per_bank):
                    count = min(per_bank, N_TILES - c0)
                    banks[i].append((psum.tile([P, count, width], F32, name="acc", tag=tag, bufs=bufs), c0, count))
            for bank, c0, count in banks[i]:
                for k in range(count):
                    ns = slice(P * (c0 + k), P * (c0 + k + 1))
                    nc.tensor.matmul_mx(
                        out=bank[:, k, :],
                        lhsT=w2_w[b][:, ns].bitcast(FP8X4),
                        lhsT_scale=w2_s[b][:, ns],
                        rhs=x_w[b][:, cols].bitcast(FP8X4),
                        rhs_scale=x_s[b][:, cols],
                        start=(b == 0 and k == 0),
                        stop=(b == PASSES - 1 and k == count - 1),
                    )

        def store(i, on_vector):
            width = CHUNKS[i]
            res = reused("res", [P, N_TILES, width], F32, ("w1_raw0", "w1_raw1", "weight_a", "weight_b")[i])
            for bank, c0, count in banks[i]:
                if on_vector:
                    nc.vector.tensor_tensor(
                        out=res[:, c0 : c0 + count, :],
                        in0=bank[:],
                        in1=tester_col[:, c0 : c0 + count].unsqueeze(2).to_broadcast([P, count, width]),
                        op=ALU.add,
                    )
                else:
                    for k in range(count):
                        c = c0 + k
                        nc.scalar.activation(
                            out=res[:, c, :], in_=bank[:, k, :], func=ACT.Identity, bias=tester_col[:, c : c + 1], scale=1.0
                        )
            nc.sync.dma_start(out=out_rows[:, :, starts[i] : starts[i] + width], in_=res[:])

        round_w1(0)
        nc.scalar.activation(out=gain_abs[:], in_=gain_raw[:].rearrange("p b t -> p (b t)"), func=ACT.Abs)
        nc.scalar.activation(out=gain_w1[:, :PACK], in_=gain_abs[:, :PACK], func=ACT.Copy)
        nc.scalar.activation(out=gain_w1[:, PACK:], in_=gain_abs[:, PACK:], func=ACT.Copy, scale=-1.0)
        quantise_w1(0)
        pick_words(3)
        weight = reused("weight", [P, M], F32, "table")
        nc.gpsimd.tensor_tensor(out=weight[:], in0=weight_a[:], in1=weight_b[:], op=ALU.mult)
        products(0)
        products(1)
        round_w1(1)
        larger(0, range(4))
        quantise_w1(1)

        x0 = held("x0", [P, PACK, M], F32)
        x1 = {0: held("x1_0", [P, PACK, CHUNKS[0]], F32)}
        x0_bf = []
        for s in range(SLICES):
            b, t = divmod(s, PACK)
            half = (M, CHUNKS[0])[b] // 2
            dst = (x0, x1[0])[b]
            if s + 2 < SLICES:
                products(s + 2)
            for block in TURNED_AT.get(s, ()):
                turned_products(block)
            if PACK <= s + 1 < SLICES:
                turn_back(s + 1)
            if s in (2, 3):
                interleave(w2_bf[s - 2][:], w2_raw[s - 2][:], nc.scalar.copy)
            if s in (4, 5):
                x0_bf.append(round_x(x0[:, :, BANK * (s - 4) : BANK * (s - 3)], nc.scalar.copy, ("weight_a", "weight_b")[s - 4]))
            larger(s + 1, (0, 1))
            xas = [reused("xa", [P, half], F32, f"staged{(s + 1) % 2}{i}") for i in range(2)]
            for i in range(2):
                seed_side(s, half * i, xas[i])
            larger(s + 1, (2, 3))
            for i in range(2):
                pollen_side(s, half * i, xas[i], dst[:, t, half * i : half * (i + 1)])
            if s in (4, 5):
                quantise_w2(s - 4)
            if s in (6, 7):
                quantise_x(0, BANK * (s - 6), x0_bf[s - 6])

        for i in range(len(CHUNKS)):
            score_pass(0, i)

        def crosses(i, ts, buffers):
            xas = [reused("xa", [P, CHUNKS[i]], F32, buffer) for buffer in buffers]
            for t, xa in zip(ts, xas):
                seed_side(PACK + t, starts[i], xa)
            for t, xa in zip(ts, xas):
                pollen_side(PACK + t, starts[i], xa, x1[i][:, t, :])

        for i in range(1, len(CHUNKS)):
            x1[i] = held(f"x1_{i}", [P, PACK, CHUNKS[i]], F32)
        half = CHUNKS[0] // 2
        bf0 = [round_x(x1[0][:, :, half * i : half * (i + 1)], nc.scalar.copy, f"tail0{i}") for i in range(2)]
        crosses(1, (0, 1), ("staged00", "staged01"))
        for i in range(2):
            quantise_x(1, half * i, bf0[i])
        score_pass(1, 0)
        crosses(1, (2, 3), ("tail00", "tail01"))
        bf1 = round_x(x1[1][:], nc.scalar.copy, "tail1")
        store(0, False)
        crosses(2, (0, 1), ("tail00", "tail01"))
        crosses(2, (2, 3), ("tail00", "tail01"))
        bf2 = round_x(x1[2][:], nc.scalar.copy, "tail2")
        quantise_x(1, starts[1], bf1)
        score_pass(1, 1)
        crosses(3, (0, 1), ("tail1", "tail01"))
        store(1, False)
        quantise_x(1, starts[2], bf2)
        score_pass(1, 2)
        crosses(3, (2, 3), ("tail2", "tail1"))
        store(2, False)
        bf3 = round_x(x1[3][:], nc.vector.tensor_copy, "tail3")
        quantise_x(1, starts[3], bf3)
        score_pass(1, 3)
        store(3, True)
